import numpy as np
import ml_dtypes


def mxq(x, axis, fmt="e4m3"):
    dtype, down = {"e4m3": (ml_dtypes.float8_e4m3fn, 7), "e5m2": (ml_dtypes.float8_e5m2, 14)}[fmt]
    v = np.moveaxis(np.asarray(x, np.float32).astype(ml_dtypes.bfloat16).astype(np.float64), axis, -1)
    blocks = v.reshape(v.shape[:-1] + (-1, 32))
    amax = np.abs(blocks).max(-1, keepdims=True)
    byte = np.maximum(np.where(amax > 0, np.frexp(amax)[1] - 1 + 127, 0) - down, 1)
    scale = np.exp2(byte - 127.0)
    codes = (blocks / scale).astype(np.float32).astype(dtype).astype(np.float64)
    return np.moveaxis((codes * scale).reshape(v.shape), -1, axis)


WIDE = False


def mx_kscale(k):
    if not WIDE:
        return np.ones(k)
    levels = np.array([10, -10, 5, -5, 0])
    if k % 512:
        return np.exp2(np.random.permutation(np.resize(levels, k // 32))).repeat(32)
    a = np.empty((k // 512, 16))
    for p in range(k // 512):
        a[p, :8] = np.random.permutation(np.resize(levels, 8))
        for g in range(8):
            far = levels[np.abs(levels - a[p, g]) >= 10]
            a[p, g + 8] = far[np.random.randint(len(far))]
    return np.exp2(a.ravel()).repeat(32)


def f64(x):
    return np.asarray(x).astype(np.float64)


def striped(idx):
    return np.tile(np.asarray(idx).reshape(-1, 16).T, (8, 1)).astype(np.uint16)


def unstriped(offs):
    return offs[:16].T.reshape(-1).astype(np.int64)


E2M1 = np.array([0.0, 0.5, 1.0, 1.5, 2.0, 3.0, 4.0, 6.0, -0.0, -0.5, -1.0, -1.5, -2.0, -3.0, -4.0, -6.0])


def pack_weight(w, fmt):
    k, n = w.shape
    w = f64(np.asarray(w, np.float32).astype(ml_dtypes.bfloat16)).reshape(k // 32, 32, n)
    amax = np.abs(w).max(1)
    if fmt == "e4m3":
        byte = np.frexp(amax)[1] - 1 + 127 - 7
    else:
        mant, ex = np.frexp(amax / 6.0)
        byte = np.where(mant > 0.5, ex, ex - 1) + 127
    byte = np.clip(np.where(amax > 0, byte, 1), 1, 254)
    scaled = (w * np.exp2(127.0 - byte)[:, None, :]).reshape(k, n).astype(np.float32)
    by_word = np.ascontiguousarray(scaled.reshape(k // 512, 128, 4, n).transpose(0, 1, 3, 2))
    if fmt == "e4m3":
        words = by_word.astype(ml_dtypes.float8_e4m3fn).view(np.uint8)
    else:
        c = by_word.astype(ml_dtypes.float4_e2m1fn).view(np.uint8) & 0xF
        words = (c[..., 0::2] | (c[..., 1::2] << 4)).reshape(k // 512, 128, 2 * n)
    return np.ascontiguousarray(words), np.ascontiguousarray(byte.astype(np.uint8).reshape(k // 512, 16, n))


def unpack_weight(words, scales, fmt):
    g, _, n = scales.shape
    words = np.ascontiguousarray(words).reshape(g, 128, n, -1)
    if fmt == "e4m3":
        vals = words.view(ml_dtypes.float8_e4m3fn).astype(np.float64)
    else:
        nib = np.empty((g, 128, n, 4), np.uint8)
        nib[..., 0::2] = words & 0xF
        nib[..., 1::2] = words >> 4
        vals = E2M1[nib]
    vals = vals * np.repeat(np.exp2(scales.astype(np.float64) - 127.0), 8, axis=1)[..., None]
    return vals.transpose(0, 1, 3, 2).reshape(g * 512, n)


D, E, T, R, I, Q = 512, 512, 2048, 1024, 512, 128


def setup_inputs():
    n = np.random.standard_normal
    idx = np.random.permutation(T)[:R]
    idx2 = np.random.permutation(R)[:I]
    fd = mx_kscale(D)
    fe = mx_kscale(E)
    keysp = pack_weight(n((D, T)) / fd[:, None], "e4m3")
    valsp = pack_weight(n((E, T)) / fe[:, None], "e4m3")
    return {
        "query": (n((D, Q)) * 0.6 / np.sqrt(D) * fd[:, None]).astype(np.float32),
        "keys_words": keysp[0],
        "keys_scales": keysp[1],
        "gout": (n((E, Q)) * 1 / np.sqrt(E) * fe[:, None]).astype(np.float32),
        "vals_words": valsp[0],
        "vals_scales": valsp[1],
        "lse": (np.random.uniform(6.2, 6.5, (Q, 1))).astype(np.float32),
        "delta": (np.random.uniform(-0.3, 0.3, (Q, 1))).astype(np.float32),
        "old": (0.5 * n((Q, R))).astype(np.float32),
        "fade": (np.random.uniform(0.5, 1.0, (1, R))).astype(np.float32),
        "offs": striped(idx),
        "offs2": striped(idx2),
    }


def reference(query, keys_words, keys_scales, gout, vals_words, vals_scales, lse, delta, old, fade, offs, offs2):
    idx = unstriped(offs)
    idx2 = unstriped(offs2)
    keysu = unpack_weight(keys_words, keys_scales, "e4m3")
    valsu = unpack_weight(vals_words, vals_scales, "e4m3")
    queryq = mxq(f64(query), 0, "e4m3")
    keysidxg = keysu[:, idx]
    a = queryq.T @ keysidxg
    goutq = mxq(f64(gout), 0, "e4m3")
    valsidxg = valsu[:, idx]
    dp = goutq.T @ valsidxg
    ds = np.exp(a[:, idx2] - f64(lse)) * (dp[:, idx2] - f64(delta)) * 512.0
    df = np.zeros((Q, R))
    df[:, idx2] = ds
    y = f64(old) * f64(fade) + df
    return y

@@ -1,0 +1,145 @@
+import math
+from contextlib import ExitStack
+
+import concourse.mybir as mybir
+from concourse.masks import make_identity
+
+D, E, T, R, I, Q = 512, 512, 2048, 1024, 512, 128
+FLOPS = 2 * Q * R * (D + E)
+
+F32 = mybir.dt.float32
+BF16 = mybir.dt.bfloat16
+I32 = mybir.dt.int32
+U32 = mybir.dt.uint32
+U16 = mybir.dt.uint16
+U8 = mybir.dt.uint8
+FP8X4 = mybir.dt.float8_e4m3fn_x4
+ALU = mybir.AluOpType
+ACT = mybir.ActivationFunctionType
+
+P = 128
+PACK = 4
+BANK = 512
+GROUP = 16
+
+
+def tile_attend_gresident_kernel(tc, query, keys_words, keys_scales, gout, vals_words, vals_scales,
+                                  lse, delta, old, fade, offs, offs2, out):
+    nc = tc.nc
+    with ExitStack() as ctx:
+        sb = ctx.enter_context(tc.tile_pool(name="sb", bufs=1))
+        ps = ctx.enter_context(tc.psum_pool(name="ps", bufs=1))
+
+        offs_t = sb.tile([P, R // GROUP], U16)
+        offs2_t = sb.tile([P, I // GROUP], U16)
+        ks_pool = sb.tile([P, T], U8)
+        vs_pool = sb.tile([P, T], U8)
+        kw_pool = sb.tile([P, T], U32)
+        vw_pool = sb.tile([P, T], U32, tag="vw_then_scores")
+        q_raw = sb.tile([P, PACK, Q], F32)
+        g_raw = sb.tile([P, PACK, Q], F32)
+        lse_t = sb.tile([P, 1], F32)
+        delta_t = sb.tile([P, 1], F32)
+        fade_cols = sb.tile([P, 2, PACK], F32)
+        old_t = sb.tile([P, R], F32)
+        a_sb = sb.tile([P, R], F32, tag="a_then_faded")
+        dp_sb = sb.tile([P, R], F32)
+        df = sb.tile([P, R], F32)
+        ident = sb.tile([P, P], F32)
+        warm = sb.tile([P, 1], F32)
+
+        nc.vector.memset(vs_pool[:].bitcast(I32), 0)
+        nc.vector.memset(df[:], 0.0)
+        make_identity(nc, ident[:])
+        nc.scalar.activation(warm[:], df[:, 0:1], ACT.Exp)
+
+        nc.sync.dma_start(offs_t[:], offs)
+        for quad in range(4):
+            rows = keys_scales[0, 4 * quad : 4 * quad + 4, :].bitcast(I32)
+            nc.sync.dma_start(ks_pool[32 * quad : 32 * quad + 32, :].bitcast(I32),
+                              rows.unsqueeze(0).to_broadcast([8, 4, T // 4]))
+        nc.sync.dma_start(kw_pool[:].bitcast(I32), keys_words[0].rearrange("p t j -> p (t j)").bitcast(I32))
+        nc.sync.dma_start(q_raw[:], query.rearrange("(p j) q -> p j q", j=PACK))
+        nc.sync.dma_start(g_raw[:], gout.rearrange("(p j) q -> p j q", j=PACK))
+        for quad in range(4):
+            nc.sync.dma_start(vs_pool[32 * quad : 32 * quad + 4, :].bitcast(I32),
+                              vals_scales[0, 4 * quad : 4 * quad + 4, :].bitcast(I32))
+        nc.sync.dma_start(vw_pool[:].bitcast(I32), vals_words[0].rearrange("p t j -> p (t j)").bitcast(I32))
+        nc.sync.dma_start(offs2_t[:], offs2)
+        nc.sync.dma_start(lse_t[:], lse)
+        nc.sync.dma_start(delta_t[:], delta)
+        nc.sync.dma_start(fade_cols[:], fade.rearrange("o (h n c) -> n (o h) c", h=2, c=PACK))
+        nc.sync.dma_start(old_t[:], old)
+
+        ks = sb.tile([P, R], U8, align_bytes=64)
+        kw = sb.tile([P, R], U32, align_bytes=64)
+        vs = sb.tile([P, R], U8, align_bytes=64)
+        vw = sb.tile([P, R], U32, align_bytes=64)
+        nc.vector.tensor_copy(ks[:], ks_pool[:].indirect(offs_t[:]))
+        nc.vector.tensor_copy(kw[:], kw_pool[:].indirect(offs_t[:]))
+
+        def quantize(raw, name):
+            grouped = sb.tile([P, Q, PACK], BF16, align_bytes=64, name=name + "_bf16")
+            codes = sb.tile([P, Q], U32, align_bytes=64, name=name + "_codes")
+            scales = sb.tile([P, Q], U8, align_bytes=64, name=name + "_scales")
+            nc.scalar.copy(grouped[:], raw[:].rearrange("p j q -> p q j"))
+            nc.vector.quantize_mx(out=codes[:].bitcast(FP8X4), scales=scales[:],
+                                  in_=grouped[:].rearrange("p q j -> p (q j)"))
+            return codes, scales
+
+        q_codes, q_scales = quantize(q_raw, "q")
+        g_codes, g_scales = quantize(g_raw, "g")
+
+        def product(dst, codes, scales, words, bytes_, c0, c1, name):
+            acc = ps.tile([P, c1 - c0], F32, name=name)
+            nc.tensor.matmul_mx(out=acc[:], lhsT=codes[:].bitcast(FP8X4), lhsT_scale=scales[:],
+                                rhs=words[:, c0:c1].bitcast(FP8X4), rhs_scale=bytes_[:, c0:c1],
+                                start=True, stop=True)
+            nc.scalar.copy(dst[:, c0:c1], acc[:])
+
+        for h in range(2):
+            product(a_sb, q_codes, q_scales, kw, ks, h * BANK, (h + 1) * BANK, "a%d" % h)
+
+        bias = sb.tile([P, 1], F32)
+        nc.scalar.activation(bias[:], lse_t[:], ACT.Copy, scale=-1.0, bias=math.log(512.0))
+        delta_wide = sb.tile([P, I], F32)
+        nc.scalar.copy(delta_wide[:], delta_t[:].to_broadcast([P, I]))
+
+        old_turned = []
+        for h in range(2):
+            bank = ps.tile([P, PACK, Q], F32, name="old_turned%d" % h)
+            for c in range(PACK):
+                nc.tensor.transpose(bank[:, c, :], old_t[:, h * BANK + c : (h + 1) * BANK : PACK], ident[:])
+            old_turned.append(bank)
+
+        nc.vector.tensor_copy(vs[:], vs_pool[:].indirect(offs_t[:]))
+        for c0, c1 in ((0, 512), (512, 768), (768, 1024)):
+            nc.vector.tensor_copy(vw[:, c0:c1], vw_pool[:].indirect(offs_t[:, c0 // GROUP : c1 // GROUP]))
+            product(dp_sb, g_codes, g_scales, vw, vs, c0, c1, "dp%d" % c0)
+
+        scores = sb.tile([P, I], F32, tag="vw_then_scores")
+        nc.vector.tensor_copy(scores[:], a_sb[:].indirect(offs2_t[:]))
+        weights = sb.tile([P, I], F32)
+        nc.scalar.activation(weights[:], scores[:], ACT.Exp, bias=bias[:])
+
+        faded_turned = sb.tile([P, 2, PACK, Q], F32, tag="a_then_faded")
+        faded = []
+        for h in range(2):
+            bank = ps.tile([P, PACK, P], F32, name="a%d" % h)
+            for c in range(PACK):
+                nc.scalar.activation(faded_turned[:, h, c, :], old_turned[h][:, c, :], ACT.Copy,
+                                     scale=fade_cols[:, h, c : c + 1])
+                nc.tensor.transpose(bank[:, c, :], faded_turned[:, h, c, :], ident[:])
+            faded.append(bank)
+
+        centred = sb.tile([P, I], F32)
+        nc.vector.tensor_tensor(centred[:], dp_sb[:].indirect(offs2_t[:]), delta_wide[:], ALU.subtract)
+        nc.vector.tensor_tensor(df[:].indirect(offs2_t[:]), centred[:], weights[:], ALU.mult)
+
+        result = sb.tile([P, R], F32)
+        for h in range(2):
+            cols = slice(h * BANK, (h + 1) * BANK)
+            nc.vector.tensor_tensor(result[:, cols].rearrange("p (n c) -> p n c", c=PACK),
+                                    df[:, cols].rearrange("p (n c) -> p n c", c=PACK),
+                                    faded[h][:].rearrange("p c n -> p n c"), ALU.add)
+            nc.sync.dma_start(out[:, cols], result[:, cols])

@@ -35,7 +35,7 @@ def tile_attend_gresident_kernel(tc, query, keys_words, keys_scales, gout, vals_
         ks_pool = sb.tile([P, T], U8)
         vs_pool = sb.tile([P, T], U8)
         kw_pool = sb.tile([P, T], U32)
-        vw_pool = sb.tile([P, T], U32, tag="vw_then_scores")
+        vw_pool = sb.tile([P, T], U32)
         q_raw = sb.tile([P, PACK, Q], F32)
         g_raw = sb.tile([P, PACK, Q], F32)
         lse_t = sb.tile([P, 1], F32)
@@ -48,7 +48,7 @@ def tile_attend_gresident_kernel(tc, query, keys_words, keys_scales, gout, vals_
         ident = sb.tile([P, P], F32)
         warm = sb.tile([P, 1], F32)
 
-        nc.vector.memset(vs_pool[:].bitcast(I32), 0)
+        nc.gpsimd.memset(vs_pool[:].bitcast(I32), 0)
         nc.vector.memset(df[:], 0.0)
         make_identity(nc, ident[:])
         nc.scalar.activation(warm[:], df[:, 0:1], ACT.Exp)
@@ -59,11 +59,11 @@ def tile_attend_gresident_kernel(tc, query, keys_words, keys_scales, gout, vals_
             nc.sync.dma_start(ks_pool[32 * quad : 32 * quad + 32, :].bitcast(I32),
                               rows.unsqueeze(0).to_broadcast([8, 4, T // 4]))
         nc.sync.dma_start(kw_pool[:].bitcast(I32), keys_words[0].rearrange("p t j -> p (t j)").bitcast(I32))
-        nc.sync.dma_start(q_raw[:], query.rearrange("(p j) q -> p j q", j=PACK))
-        nc.sync.dma_start(g_raw[:], gout.rearrange("(p j) q -> p j q", j=PACK))
         for quad in range(4):
             nc.sync.dma_start(vs_pool[32 * quad : 32 * quad + 4, :].bitcast(I32),
                               vals_scales[0, 4 * quad : 4 * quad + 4, :].bitcast(I32))
+        nc.sync.dma_start(q_raw[:], query.rearrange("(p j) q -> p j q", j=PACK))
+        nc.sync.dma_start(g_raw[:], gout.rearrange("(p j) q -> p j q", j=PACK))
         nc.sync.dma_start(vw_pool[:].bitcast(I32), vals_words[0].rearrange("p t j -> p (t j)").bitcast(I32))
         nc.sync.dma_start(offs2_t[:], offs2)
         nc.sync.dma_start(lse_t[:], lse)
@@ -74,31 +74,30 @@ def tile_attend_gresident_kernel(tc, query, keys_words, keys_scales, gout, vals_
         ks = sb.tile([P, R], U8, align_bytes=64)
         kw = sb.tile([P, R], U32, align_bytes=64)
         vs = sb.tile([P, R], U8, align_bytes=64)
-        vw = sb.tile([P, R], U32, align_bytes=64)
         nc.vector.tensor_copy(ks[:], ks_pool[:].indirect(offs_t[:]))
         nc.vector.tensor_copy(kw[:], kw_pool[:].indirect(offs_t[:]))
 
-        def quantize(raw, name):
-            grouped = sb.tile([P, Q, PACK], BF16, align_bytes=64, name=name + "_bf16")
-            codes = sb.tile([P, Q], U32, align_bytes=64, name=name + "_codes")
-            scales = sb.tile([P, Q], U8, align_bytes=64, name=name + "_scales")
-            nc.scalar.copy(grouped[:], raw[:].rearrange("p j q -> p q j"))
-            nc.vector.quantize_mx(out=codes[:].bitcast(FP8X4), scales=scales[:],
-                                  in_=grouped[:].rearrange("p q j -> p (q j)"))
-            return codes, scales
+        nc.vector.tensor_copy(vs[:], vs_pool[:].indirect(offs_t[:]))
 
-        q_codes, q_scales = quantize(q_raw, "q")
-        g_codes, g_scales = quantize(g_raw, "g")
+        grouped = sb.tile([P, 2, Q, PACK], BF16, align_bytes=64)
+        codes = sb.tile([P, 2 * Q], U32, align_bytes=64)
+        scales = sb.tile([P, 2 * Q], U8, align_bytes=64)
+        nc.scalar.copy(grouped[:, 0], q_raw[:].rearrange("p j q -> p q j"))
+        nc.scalar.copy(grouped[:, 1], g_raw[:].rearrange("p j q -> p q j"))
+        nc.vector.quantize_mx(out=codes[:].bitcast(FP8X4), scales=scales[:],
+                              in_=grouped[:].rearrange("p o q j -> p (o q j)"))
+        q_codes, q_scales = codes[:, :Q], scales[:, :Q]
+        g_codes, g_scales = codes[:, Q:], scales[:, Q:]
 
         def product(dst, codes, scales, words, bytes_, c0, c1, name):
             acc = ps.tile([P, c1 - c0], F32, name=name)
-            nc.tensor.matmul_mx(out=acc[:], lhsT=codes[:].bitcast(FP8X4), lhsT_scale=scales[:],
-                                rhs=words[:, c0:c1].bitcast(FP8X4), rhs_scale=bytes_[:, c0:c1],
+            nc.tensor.matmul_mx(out=acc[:], lhsT=codes.bitcast(FP8X4), lhsT_scale=scales,
+                                rhs=words.bitcast(FP8X4), rhs_scale=bytes_[:, c0:c1],
                                 start=True, stop=True)
             nc.scalar.copy(dst[:, c0:c1], acc[:])
 
         for h in range(2):
-            product(a_sb, q_codes, q_scales, kw, ks, h * BANK, (h + 1) * BANK, "a%d" % h)
+            product(a_sb, q_codes, q_scales, kw[:, h * BANK : (h + 1) * BANK], ks, h * BANK, (h + 1) * BANK, "a%d" % h)
 
         bias = sb.tile([P, 1], F32)
         nc.scalar.activation(bias[:], lse_t[:], ACT.Copy, scale=-1.0, bias=math.log(512.0))
@@ -112,15 +111,18 @@ def tile_attend_gresident_kernel(tc, query, keys_words, keys_scales, gout, vals_
                 nc.tensor.transpose(bank[:, c, :], old_t[:, h * BANK + c : (h + 1) * BANK : PACK], ident[:])
             old_turned.append(bank)
 
-        nc.vector.tensor_copy(vs[:], vs_pool[:].indirect(offs_t[:]))
         for c0, c1 in ((0, 512), (512, 768), (768, 1024)):
-            nc.vector.tensor_copy(vw[:, c0:c1], vw_pool[:].indirect(offs_t[:, c0 // GROUP : c1 // GROUP]))
-            product(dp_sb, g_codes, g_scales, vw, vs, c0, c1, "dp%d" % c0)
+            vw = sb.tile([P, c1 - c0], U32, align_bytes=64, name="vw%d" % c0)
+            nc.vector.tensor_copy(vw[:], vw_pool[:].indirect(offs_t[:, c0 // GROUP : c1 // GROUP]))
+            product(dp_sb, g_codes, g_scales, vw[:], vs, c0, c1, "dp%d" % c0)
 
-        scores = sb.tile([P, I], F32, tag="vw_then_scores")
-        nc.vector.tensor_copy(scores[:], a_sb[:].indirect(offs2_t[:]))
+        scores = sb.tile([P, I], F32, align_bytes=64, name="vw0")
         weights = sb.tile([P, I], F32)
+        nc.vector.tensor_copy(scores[:], a_sb[:].indirect(offs2_t[:]))
         nc.scalar.activation(weights[:], scores[:], ACT.Exp, bias=bias[:])
+        centred = sb.tile([P, I], F32)
+        nc.vector.tensor_tensor(centred[:], dp_sb[:].indirect(offs2_t[:]), delta_wide[:], ALU.subtract)
+        nc.vector.tensor_tensor(df[:].indirect(offs2_t[:]), centred[:], weights[:], ALU.mult)
 
         faded_turned = sb.tile([P, 2, PACK, Q], F32, tag="a_then_faded")
         faded = []
@@ -132,14 +134,10 @@ def tile_attend_gresident_kernel(tc, query, keys_words, keys_scales, gout, vals_
                 nc.tensor.transpose(bank[:, c, :], faded_turned[:, h, c, :], ident[:])
             faded.append(bank)
 
-        centred = sb.tile([P, I], F32)
-        nc.vector.tensor_tensor(centred[:], dp_sb[:].indirect(offs2_t[:]), delta_wide[:], ALU.subtract)
-        nc.vector.tensor_tensor(df[:].indirect(offs2_t[:]), centred[:], weights[:], ALU.mult)
-
-        result = sb.tile([P, R], F32)
-        for h in range(2):
-            cols = slice(h * BANK, (h + 1) * BANK)
-            nc.vector.tensor_tensor(result[:, cols].rearrange("p (n c) -> p n c", c=PACK),
-                                    df[:, cols].rearrange("p (n c) -> p n c", c=PACK),
-                                    faded[h][:].rearrange("p c n -> p n c"), ALU.add)
-            nc.sync.dma_start(out[:, cols], result[:, cols])
+        for (c0, c1), queue in (((0, 256), nc.sync), ((256, 512), nc.scalar), ((512, 768), nc.sync), ((768, 1024), nc.scalar)):
+            h, n0, n1 = c0 // BANK, c0 % BANK // PACK, ((c1 - 1) % BANK + 1) // PACK
+            result = sb.tile([P, c1 - c0], F32, name="result%d" % c0)
+            nc.vector.tensor_tensor(result[:].rearrange("p (n c) -> p n c", c=PACK),
+                                    df[:, c0:c1].rearrange("p (n c) -> p n c", c=PACK),
+                                    faded[h][:, :, n0:n1].rearrange("p c n -> p n c"), ALU.add)
+            queue.dma_start(out[:, c0:c1], result[:])

@@ -21,6 +21,7 @@ P = 128
 PACK = 4
 BANK = 512
 GROUP = 16
+BLOCKS = R // P
 
 
 def tile_attend_gresident_kernel(tc, query, keys_words, keys_scales, gout, vals_words, vals_scales,
@@ -40,7 +41,7 @@ def tile_attend_gresident_kernel(tc, query, keys_words, keys_scales, gout, vals_
         g_raw = sb.tile([P, PACK, Q], F32)
         lse_t = sb.tile([P, 1], F32)
         delta_t = sb.tile([P, 1], F32)
-        fade_cols = sb.tile([P, 2, PACK], F32)
+        fade_rows = sb.tile([P, P], F32)
         old_t = sb.tile([P, R], F32)
         a_sb = sb.tile([P, R], F32, tag="a_then_faded")
         dp_sb = sb.tile([P, R], F32)
@@ -68,7 +69,7 @@ def tile_attend_gresident_kernel(tc, query, keys_words, keys_scales, gout, vals_
         nc.sync.dma_start(offs2_t[:], offs2)
         nc.sync.dma_start(lse_t[:], lse)
         nc.sync.dma_start(delta_t[:], delta)
-        nc.sync.dma_start(fade_cols[:], fade.rearrange("o (h n c) -> n (o h) c", h=2, c=PACK))
+        nc.sync.dma_start(fade_rows[:], fade.rearrange("o (b n) -> o b n", n=P).to_broadcast([P // BLOCKS, BLOCKS, P]))
         nc.sync.dma_start(old_t[:], old)
 
         ks = sb.tile([P, R], U8, align_bytes=64)
@@ -104,12 +105,10 @@ def tile_attend_gresident_kernel(tc, query, keys_words, keys_scales, gout, vals_
         delta_wide = sb.tile([P, I], F32)
         nc.scalar.copy(delta_wide[:], delta_t[:].to_broadcast([P, I]))
 
-        old_turned = []
-        for h in range(2):
-            bank = ps.tile([P, PACK, Q], F32, name="old_turned%d" % h)
-            for c in range(PACK):
-                nc.tensor.transpose(bank[:, c, :], old_t[:, h * BANK + c : (h + 1) * BANK : PACK], ident[:])
-            old_turned.append(bank)
+        fade_turned = ps.tile([P, P], F32)
+        nc.tensor.transpose(fade_turned[:], fade_rows[:], ident[:])
+        fade_cols = sb.tile([P, BLOCKS], F32)
+        nc.scalar.copy(fade_cols[:], fade_turned[:, :BLOCKS])
 
         for c0, c1 in ((0, 512), (512, 768), (768, 1024)):
             vw = sb.tile([P, c1 - c0], U32, align_bytes=64, name="vw%d" % c0)
@@ -124,20 +123,26 @@ def tile_attend_gresident_kernel(tc, query, keys_words, keys_scales, gout, vals_
         nc.vector.tensor_tensor(centred[:], dp_sb[:].indirect(offs2_t[:]), delta_wide[:], ALU.subtract)
         nc.vector.tensor_tensor(df[:].indirect(offs2_t[:]), centred[:], weights[:], ALU.mult)
 
-        faded_turned = sb.tile([P, 2, PACK, Q], F32, tag="a_then_faded")
+        old_turned = []
+        for h in range(2):
+            bank = ps.tile([P, PACK, Q], F32, name="dp%d" % (512 + 256 * h))
+            for c in range(PACK):
+                b = h * PACK + c
+                nc.tensor.transpose(bank[:, c, :], old_t[:, b * P : (b + 1) * P], ident[:])
+            old_turned.append(bank)
+        faded_turned = sb.tile([P, BLOCKS, Q], F32, tag="a_then_faded")
         faded = []
         for h in range(2):
-            bank = ps.tile([P, PACK, P], F32, name="a%d" % h)
+            bank = ps.tile([P, BANK], F32, name="a%d" % h)
             for c in range(PACK):
-                nc.scalar.activation(faded_turned[:, h, c, :], old_turned[h][:, c, :], ACT.Copy,
-                                     scale=fade_cols[:, h, c : c + 1])
-                nc.tensor.transpose(bank[:, c, :], faded_turned[:, h, c, :], ident[:])
+                b = h * PACK + c
+                nc.scalar.activation(faded_turned[:, b, :], old_turned[h][:, c, :], ACT.Copy,
+                                     scale=fade_cols[:, b : b + 1])
+                nc.tensor.transpose(bank[:, c * P : (c + 1) * P], faded_turned[:, b, :], ident[:])
             faded.append(bank)
 
         for (c0, c1), queue in (((0, 256), nc.sync), ((256, 512), nc.scalar), ((512, 768), nc.sync), ((768, 1024), nc.scalar)):
-            h, n0, n1 = c0 // BANK, c0 % BANK // PACK, ((c1 - 1) % BANK + 1) // PACK
             result = sb.tile([P, c1 - c0], F32, name="result%d" % c0)
-            nc.vector.tensor_tensor(result[:].rearrange("p (n c) -> p n c", c=PACK),
-                                    df[:, c0:c1].rearrange("p (n c) -> p n c", c=PACK),
-                                    faded[h][:, :, n0:n1].rearrange("p c n -> p n c"), ALU.add)
+            in_bank = c0 % BANK
+            nc.vector.tensor_tensor(result[:], df[:, c0:c1], faded[c0 // BANK][:, in_bank : in_bank + c1 - c0], ALU.add)
             queue.dma_start(out[:, c0:c1], result[:])

@@ -49,16 +49,18 @@ def tile_attend_gresident_kernel(tc, query, keys_words, keys_scales, gout, vals_
         ident = sb.tile([P, P], F32)
         warm = sb.tile([P, 1], F32)
 
-        nc.gpsimd.memset(vs_pool[:].bitcast(I32), 0)
+        nc.vector.memset(ks_pool[:].bitcast(I32), 0)
+        nc.vector.memset(vs_pool[:].bitcast(I32), 0)
         nc.vector.memset(df[:], 0.0)
         make_identity(nc, ident[:])
-        nc.scalar.activation(warm[:], df[:, 0:1], ACT.Exp)
+        nc.scalar.activation(warm[:], ident[:, 0:1], ACT.Exp)
 
         nc.sync.dma_start(offs_t[:], offs)
+        nc.sync.dma_start(offs2_t[:], offs2)
+        nc.sync.dma_start(lse_t[:], lse)
         for quad in range(4):
-            rows = keys_scales[0, 4 * quad : 4 * quad + 4, :].bitcast(I32)
-            nc.sync.dma_start(ks_pool[32 * quad : 32 * quad + 32, :].bitcast(I32),
-                              rows.unsqueeze(0).to_broadcast([8, 4, T // 4]))
+            nc.sync.dma_start(ks_pool[32 * quad : 32 * quad + 4, :].bitcast(I32),
+                              keys_scales[0, 4 * quad : 4 * quad + 4, :].bitcast(I32))
         nc.sync.dma_start(kw_pool[:].bitcast(I32), keys_words[0].rearrange("p t j -> p (t j)").bitcast(I32))
         for quad in range(4):
             nc.sync.dma_start(vs_pool[32 * quad : 32 * quad + 4, :].bitcast(I32),
@@ -66,8 +68,6 @@ def tile_attend_gresident_kernel(tc, query, keys_words, keys_scales, gout, vals_
         nc.sync.dma_start(q_raw[:], query.rearrange("(p j) q -> p j q", j=PACK))
         nc.sync.dma_start(g_raw[:], gout.rearrange("(p j) q -> p j q", j=PACK))
         nc.sync.dma_start(vw_pool[:].bitcast(I32), vals_words[0].rearrange("p t j -> p (t j)").bitcast(I32))
-        nc.sync.dma_start(offs2_t[:], offs2)
-        nc.sync.dma_start(lse_t[:], lse)
         nc.sync.dma_start(delta_t[:], delta)
         nc.sync.dma_start(fade_rows[:], fade.rearrange("o (b n) -> o b n", n=P).to_broadcast([P // BLOCKS, BLOCKS, P]))
         nc.sync.dma_start(old_t[:], old)

@@ -19,9 +19,15 @@ ACT = mybir.ActivationFunctionType
 
 P = 128
 PACK = 4
+QUADRANT = 32
+SCALE_ROWS = D // 32
 BANK = 512
-GROUP = 16
+LIST_ROWS = 16
 BLOCKS = R // P
+BLOCKS_A_BANK = BANK // P
+EARLY_KEY_COLUMNS = 256
+VALUE_PIECES = ((0, 512), (512, 768), (768, 1024))
+STORE_COLUMNS = 256
 
 
 def tile_attend_gresident_kernel(tc, query, keys_words, keys_scales, gout, vals_words, vals_scales,
@@ -31,14 +37,14 @@ def tile_attend_gresident_kernel(tc, query, keys_words, keys_scales, gout, vals_
         sb = ctx.enter_context(tc.tile_pool(name="sb", bufs=1))
         ps = ctx.enter_context(tc.psum_pool(name="ps", bufs=1))
 
-        offs_t = sb.tile([P, R // GROUP], U16)
-        offs2_t = sb.tile([P, I // GROUP], U16)
-        ks_pool = sb.tile([P, T], U8)
-        vs_pool = sb.tile([P, T], U8)
-        kw_pool = sb.tile([P, T], U32)
-        vw_pool = sb.tile([P, T], U32)
-        q_raw = sb.tile([P, PACK, Q], F32)
-        g_raw = sb.tile([P, PACK, Q], F32)
+        offs_t = sb.tile([P, R // LIST_ROWS], U16)
+        offs2_t = sb.tile([P, I // LIST_ROWS], U16)
+        key_scale_pool = sb.tile([P, T], U8)
+        val_scale_pool = sb.tile([P, T], U8)
+        key_word_pool = sb.tile([P, T], U32)
+        val_word_pool = sb.tile([P, T], U32)
+        query_raw = sb.tile([P, PACK, Q], F32)
+        gout_raw = sb.tile([P, PACK, Q], F32)
         lse_t = sb.tile([P, 1], F32)
         delta_t = sb.tile([P, 1], F32)
         fade_rows = sb.tile([P, P], F32)
@@ -47,102 +53,110 @@ def tile_attend_gresident_kernel(tc, query, keys_words, keys_scales, gout, vals_
         dp_sb = sb.tile([P, R], F32)
         df = sb.tile([P, R], F32)
         ident = sb.tile([P, P], F32)
-        warm = sb.tile([P, 1], F32)
 
-        nc.vector.memset(ks_pool[:].bitcast(I32), 0)
-        nc.vector.memset(vs_pool[:].bitcast(I32), 0)
+        nc.vector.memset(key_scale_pool[:].bitcast(I32), 0)
+        nc.vector.memset(ident[:], 0.0)
+        make_identity(nc, ident[:], nomemset=True)
+        nc.vector.memset(val_scale_pool[:].bitcast(I32), 0)
+        nc.vector.memset(fade_rows[:], 0.0)
         nc.vector.memset(df[:], 0.0)
-        make_identity(nc, ident[:])
-        nc.scalar.activation(warm[:], ident[:, 0:1], ACT.Exp)
 
+        def load_scale_rows(pool_tile, scale_rows):
+            for f in range(PACK):
+                nc.sync.dma_start(pool_tile[f:P:QUADRANT, :].bitcast(I32),
+                                  scale_rows[0, f:SCALE_ROWS:PACK, :].bitcast(I32))
+
+        key_words_hbm = keys_words[0].rearrange("p t j -> p (t j)").bitcast(I32)
+        val_words_hbm = vals_words[0].rearrange("p t j -> p (t j)").bitcast(I32)
         nc.sync.dma_start(offs_t[:], offs)
+        nc.sync.dma_start(delta_t[:], delta)
+        nc.sync.dma_start(key_word_pool[:, :EARLY_KEY_COLUMNS].bitcast(I32), key_words_hbm[:, :EARLY_KEY_COLUMNS])
+        load_scale_rows(key_scale_pool, keys_scales)
+        nc.sync.dma_start(key_word_pool[:, EARLY_KEY_COLUMNS:].bitcast(I32), key_words_hbm[:, EARLY_KEY_COLUMNS:])
+        load_scale_rows(val_scale_pool, vals_scales)
+        nc.sync.dma_start(query_raw[:], query.rearrange("(p j) q -> p j q", j=PACK))
+        nc.sync.dma_start(gout_raw[:], gout.rearrange("(p j) q -> p j q", j=PACK))
+        nc.sync.dma_start(val_word_pool[:].bitcast(I32), val_words_hbm)
         nc.sync.dma_start(offs2_t[:], offs2)
         nc.sync.dma_start(lse_t[:], lse)
-        for quad in range(4):
-            nc.sync.dma_start(ks_pool[32 * quad : 32 * quad + 4, :].bitcast(I32),
-                              keys_scales[0, 4 * quad : 4 * quad + 4, :].bitcast(I32))
-        nc.sync.dma_start(kw_pool[:].bitcast(I32), keys_words[0].rearrange("p t j -> p (t j)").bitcast(I32))
-        for quad in range(4):
-            nc.sync.dma_start(vs_pool[32 * quad : 32 * quad + 4, :].bitcast(I32),
-                              vals_scales[0, 4 * quad : 4 * quad + 4, :].bitcast(I32))
-        nc.sync.dma_start(q_raw[:], query.rearrange("(p j) q -> p j q", j=PACK))
-        nc.sync.dma_start(g_raw[:], gout.rearrange("(p j) q -> p j q", j=PACK))
-        nc.sync.dma_start(vw_pool[:].bitcast(I32), vals_words[0].rearrange("p t j -> p (t j)").bitcast(I32))
-        nc.sync.dma_start(delta_t[:], delta)
-        nc.sync.dma_start(fade_rows[:], fade.rearrange("o (b n) -> o b n", n=P).to_broadcast([P // BLOCKS, BLOCKS, P]))
+        nc.sync.dma_start(fade_rows[:BLOCKS, :], fade.rearrange("o (b n) -> (o b) n", n=P))
         nc.sync.dma_start(old_t[:], old)
 
-        ks = sb.tile([P, R], U8, align_bytes=64)
-        kw = sb.tile([P, R], U32, align_bytes=64)
-        vs = sb.tile([P, R], U8, align_bytes=64)
-        nc.vector.tensor_copy(ks[:], ks_pool[:].indirect(offs_t[:]))
-        nc.vector.tensor_copy(kw[:], kw_pool[:].indirect(offs_t[:]))
+        key_scales = sb.tile([P, R], U8, align_bytes=64)
+        key_words = sb.tile([P, R], U32, align_bytes=64)
+        val_scales = sb.tile([P, R], U8, align_bytes=64)
+        nc.vector.tensor_copy(key_scales[:], key_scale_pool[:].indirect(offs_t[:]))
+        nc.vector.tensor_copy(key_words[:], key_word_pool[:].indirect(offs_t[:]))
+        nc.vector.tensor_copy(val_scales[:], val_scale_pool[:].indirect(offs_t[:]))
 
-        nc.vector.tensor_copy(vs[:], vs_pool[:].indirect(offs_t[:]))
+        delta_wide = sb.tile([P, I], F32)
+        nc.scalar.activation(delta_wide[:], delta_t[:].to_broadcast([P, I]), ACT.Copy)
 
         grouped = sb.tile([P, 2, Q, PACK], BF16, align_bytes=64)
-        codes = sb.tile([P, 2 * Q], U32, align_bytes=64)
-        scales = sb.tile([P, 2 * Q], U8, align_bytes=64)
-        nc.scalar.copy(grouped[:, 0], q_raw[:].rearrange("p j q -> p q j"))
-        nc.scalar.copy(grouped[:, 1], g_raw[:].rearrange("p j q -> p q j"))
-        nc.vector.quantize_mx(out=codes[:].bitcast(FP8X4), scales=scales[:],
+        row_words = sb.tile([P, 2 * Q], U32, align_bytes=64)
+        row_scales = sb.tile([P, 2 * Q], U8, align_bytes=64)
+        nc.scalar.activation(grouped[:, 0], query_raw[:].rearrange("p j q -> p q j"), ACT.Copy)
+        nc.scalar.activation(grouped[:, 1], gout_raw[:].rearrange("p j q -> p q j"), ACT.Copy)
+        nc.vector.quantize_mx(out=row_words[:].bitcast(FP8X4), scales=row_scales[:],
                               in_=grouped[:].rearrange("p o q j -> p (o q j)"))
-        q_codes, q_scales = codes[:, :Q], scales[:, :Q]
-        g_codes, g_scales = codes[:, Q:], scales[:, Q:]
+        query_cols, gout_cols = slice(0, Q), slice(Q, 2 * Q)
 
-        def product(dst, codes, scales, words, bytes_, c0, c1, name):
-            acc = ps.tile([P, c1 - c0], F32, name=name)
-            nc.tensor.matmul_mx(out=acc[:], lhsT=codes.bitcast(FP8X4), lhsT_scale=scales,
-                                rhs=words.bitcast(FP8X4), rhs_scale=bytes_[:, c0:c1],
-                                start=True, stop=True)
-            nc.scalar.copy(dst[:, c0:c1], acc[:])
+        def product(dst, row_cols, slot_words, slot_scales, bank_tag):
+            acc = ps.tile(dst.shape, F32, name=bank_tag)
+            nc.tensor.matmul_mx(out=acc[:], lhsT=row_words[:, row_cols].bitcast(FP8X4),
+                                lhsT_scale=row_scales[:, row_cols], rhs=slot_words.bitcast(FP8X4),
+                                rhs_scale=slot_scales, start=True, stop=True)
+            nc.scalar.copy(dst, acc[:])
 
-        for h in range(2):
-            product(a_sb, q_codes, q_scales, kw[:, h * BANK : (h + 1) * BANK], ks, h * BANK, (h + 1) * BANK, "a%d" % h)
+        for h in range(R // BANK):
+            cols = slice(h * BANK, (h + 1) * BANK)
+            product(a_sb[:, cols], query_cols, key_words[:, cols], key_scales[:, cols], "a%d" % h)
 
-        bias = sb.tile([P, 1], F32)
-        nc.scalar.activation(bias[:], lse_t[:], ACT.Copy, scale=-1.0, bias=math.log(512.0))
-        delta_wide = sb.tile([P, I], F32)
-        nc.scalar.copy(delta_wide[:], delta_t[:].to_broadcast([P, I]))
+        exp_bias = sb.tile([P, 1], F32)
+        nc.scalar.activation(exp_bias[:], lse_t[:], ACT.Copy, scale=-1.0, bias=math.log(512.0))
 
         fade_turned = ps.tile([P, P], F32)
         nc.tensor.transpose(fade_turned[:], fade_rows[:], ident[:])
         fade_cols = sb.tile([P, BLOCKS], F32)
         nc.scalar.copy(fade_cols[:], fade_turned[:, :BLOCKS])
 
-        for c0, c1 in ((0, 512), (512, 768), (768, 1024)):
-            vw = sb.tile([P, c1 - c0], U32, align_bytes=64, name="vw%d" % c0)
-            nc.vector.tensor_copy(vw[:], vw_pool[:].indirect(offs_t[:, c0 // GROUP : c1 // GROUP]))
-            product(dp_sb, g_codes, g_scales, vw[:], vs, c0, c1, "dp%d" % c0)
+        for c0, c1 in VALUE_PIECES:
+            val_words = sb.tile([P, c1 - c0], U32, align_bytes=64, name="val_words%d" % c0)
+            nc.vector.tensor_copy(val_words[:],
+                                  val_word_pool[:].indirect(offs_t[:, c0 // LIST_ROWS : c1 // LIST_ROWS]))
+            product(dp_sb[:, c0:c1], gout_cols, val_words[:], val_scales[:, c0:c1], "dp%d" % c0)
 
-        scores = sb.tile([P, I], F32, align_bytes=64, name="vw0")
+        a_picked = sb.tile([P, I], F32, align_bytes=64, name="val_words%d" % VALUE_PIECES[0][0])
         weights = sb.tile([P, I], F32)
-        nc.vector.tensor_copy(scores[:], a_sb[:].indirect(offs2_t[:]))
-        nc.scalar.activation(weights[:], scores[:], ACT.Exp, bias=bias[:])
+        nc.vector.tensor_copy(a_picked[:], a_sb[:].indirect(offs2_t[:]))
+        nc.scalar.activation(weights[:], a_picked[:], ACT.Exp, bias=exp_bias[:])
         centred = sb.tile([P, I], F32)
         nc.vector.tensor_tensor(centred[:], dp_sb[:].indirect(offs2_t[:]), delta_wide[:], ALU.subtract)
         nc.vector.tensor_tensor(df[:].indirect(offs2_t[:]), centred[:], weights[:], ALU.mult)
 
         old_turned = []
-        for h in range(2):
-            bank = ps.tile([P, PACK, Q], F32, name="dp%d" % (512 + 256 * h))
-            for c in range(PACK):
-                b = h * PACK + c
-                nc.tensor.transpose(bank[:, c, :], old_t[:, b * P : (b + 1) * P], ident[:])
-            old_turned.append(bank)
+        for h in range(R // BANK):
+            turned_bank = ps.tile([P, BLOCKS_A_BANK, Q], F32, name="dp%d" % VALUE_PIECES[h + 1][0])
+            for c in range(BLOCKS_A_BANK):
+                b = h * BLOCKS_A_BANK + c
+                nc.tensor.transpose(turned_bank[:, c, :], old_t[:, b * P : (b + 1) * P], ident[:])
+            old_turned.append(turned_bank)
         faded_turned = sb.tile([P, BLOCKS, Q], F32, tag="a_then_faded")
         faded = []
-        for h in range(2):
-            bank = ps.tile([P, BANK], F32, name="a%d" % h)
-            for c in range(PACK):
-                b = h * PACK + c
+        for h in range(R // BANK):
+            faded_bank = ps.tile([P, BANK], F32, name="a%d" % h)
+            for c in range(BLOCKS_A_BANK):
+                b = h * BLOCKS_A_BANK + c
                 nc.scalar.activation(faded_turned[:, b, :], old_turned[h][:, c, :], ACT.Copy,
                                      scale=fade_cols[:, b : b + 1])
-                nc.tensor.transpose(bank[:, c * P : (c + 1) * P], faded_turned[:, b, :], ident[:])
-            faded.append(bank)
+                nc.tensor.transpose(faded_bank[:, c * P : (c + 1) * P], faded_turned[:, b, :], ident[:])
+            faded.append(faded_bank)
 
-        for (c0, c1), queue in (((0, 256), nc.sync), ((256, 512), nc.scalar), ((512, 768), nc.sync), ((768, 1024), nc.scalar)):
-            result = sb.tile([P, c1 - c0], F32, name="result%d" % c0)
+        for piece in range(R // STORE_COLUMNS):
+            c0 = piece * STORE_COLUMNS
             in_bank = c0 % BANK
-            nc.vector.tensor_tensor(result[:], df[:, c0:c1], faded[c0 // BANK][:, in_bank : in_bank + c1 - c0], ALU.add)
-            queue.dma_start(out[:, c0:c1], result[:])
+            result = sb.tile([P, STORE_COLUMNS], F32, name="result%d" % piece)
+            nc.vector.tensor_tensor(result[:], df[:, c0 : c0 + STORE_COLUMNS],
+                                    faded[c0 // BANK][:, in_bank : in_bank + STORE_COLUMNS], ALU.add)
+            queue = (nc.sync, nc.scalar)[piece % 2]
+            queue.dma_start(out[:, c0 : c0 + STORE_COLUMNS], result[:])

import math
from contextlib import ExitStack

import concourse.mybir as mybir
from concourse.masks import make_identity

D, E, T, R, I, Q = 512, 512, 2048, 1024, 512, 128
FLOPS = 2 * Q * R * (D + E)

F32 = mybir.dt.float32
BF16 = mybir.dt.bfloat16
I32 = mybir.dt.int32
U32 = mybir.dt.uint32
U16 = mybir.dt.uint16
U8 = mybir.dt.uint8
FP8X4 = mybir.dt.float8_e4m3fn_x4
ALU = mybir.AluOpType
ACT = mybir.ActivationFunctionType

P = 128
PACK = 4
QUADRANT = 32
SCALE_ROWS = D // 32
BANK = 512
LIST_ROWS = 16
BLOCKS = R // P
BLOCKS_A_BANK = BANK // P
EARLY_KEY_COLUMNS = 256
VALUE_PIECES = ((0, 512), (512, 768), (768, 1024))
STORE_COLUMNS = 256


def tile_attend_gresident_kernel(tc, query, keys_words, keys_scales, gout, vals_words, vals_scales,
                                  lse, delta, old, fade, offs, offs2, out):
    nc = tc.nc
    with ExitStack() as ctx:
        sb = ctx.enter_context(tc.tile_pool(name="sb", bufs=1))
        ps = ctx.enter_context(tc.psum_pool(name="ps", bufs=1))

        offs_t = sb.tile([P, R // LIST_ROWS], U16)
        offs2_t = sb.tile([P, I // LIST_ROWS], U16)
        key_scale_pool = sb.tile([P, T], U8)
        val_scale_pool = sb.tile([P, T], U8)
        key_word_pool = sb.tile([P, T], U32)
        val_word_pool = sb.tile([P, T], U32)
        query_raw = sb.tile([P, PACK, Q], F32)
        gout_raw = sb.tile([P, PACK, Q], F32)
        lse_t = sb.tile([P, 1], F32)
        delta_t = sb.tile([P, 1], F32)
        fade_rows = sb.tile([P, P], F32)
        old_t = sb.tile([P, R], F32)
        a_sb = sb.tile([P, R], F32, tag="a_then_faded")
        dp_sb = sb.tile([P, R], F32)
        df = sb.tile([P, R], F32)
        ident = sb.tile([P, P], F32)

        nc.vector.memset(key_scale_pool[:].bitcast(I32), 0)
        nc.vector.memset(ident[:], 0.0)
        make_identity(nc, ident[:], nomemset=True)
        nc.vector.memset(val_scale_pool[:].bitcast(I32), 0)
        nc.vector.memset(fade_rows[:], 0.0)
        nc.vector.memset(df[:], 0.0)

        def load_scale_rows(pool_tile, scale_rows):
            for f in range(PACK):
                nc.sync.dma_start(pool_tile[f:P:QUADRANT, :].bitcast(I32),
                                  scale_rows[0, f:SCALE_ROWS:PACK, :].bitcast(I32))

        key_words_hbm = keys_words[0].rearrange("p t j -> p (t j)").bitcast(I32)
        val_words_hbm = vals_words[0].rearrange("p t j -> p (t j)").bitcast(I32)
        nc.sync.dma_start(offs_t[:], offs)
        nc.sync.dma_start(delta_t[:], delta)
        nc.sync.dma_start(key_word_pool[:, :EARLY_KEY_COLUMNS].bitcast(I32), key_words_hbm[:, :EARLY_KEY_COLUMNS])
        load_scale_rows(key_scale_pool, keys_scales)
        nc.sync.dma_start(key_word_pool[:, EARLY_KEY_COLUMNS:].bitcast(I32), key_words_hbm[:, EARLY_KEY_COLUMNS:])
        load_scale_rows(val_scale_pool, vals_scales)
        nc.sync.dma_start(query_raw[:], query.rearrange("(p j) q -> p j q", j=PACK))
        nc.sync.dma_start(gout_raw[:], gout.rearrange("(p j) q -> p j q", j=PACK))
        nc.sync.dma_start(val_word_pool[:].bitcast(I32), val_words_hbm)
        nc.sync.dma_start(offs2_t[:], offs2)
        nc.sync.dma_start(lse_t[:], lse)
        nc.sync.dma_start(fade_rows[:BLOCKS, :], fade.rearrange("o (b n) -> (o b) n", n=P))
        nc.sync.dma_start(old_t[:], old)

        key_scales = sb.tile([P, R], U8, align_bytes=64)
        key_words = sb.tile([P, R], U32, align_bytes=64)
        val_scales = sb.tile([P, R], U8, align_bytes=64)
        nc.vector.tensor_copy(key_scales[:], key_scale_pool[:].indirect(offs_t[:]))
        nc.vector.tensor_copy(key_words[:], key_word_pool[:].indirect(offs_t[:]))
        nc.vector.tensor_copy(val_scales[:], val_scale_pool[:].indirect(offs_t[:]))

        delta_wide = sb.tile([P, I], F32)
        nc.scalar.activation(delta_wide[:], delta_t[:].to_broadcast([P, I]), ACT.Copy)

        grouped = sb.tile([P, 2, Q, PACK], BF16, align_bytes=64)
        row_words = sb.tile([P, 2 * Q], U32, align_bytes=64)
        row_scales = sb.tile([P, 2 * Q], U8, align_bytes=64)
        nc.scalar.activation(grouped[:, 0], query_raw[:].rearrange("p j q -> p q j"), ACT.Copy)
        nc.scalar.activation(grouped[:, 1], gout_raw[:].rearrange("p j q -> p q j"), ACT.Copy)
        nc.vector.quantize_mx(out=row_words[:].bitcast(FP8X4), scales=row_scales[:],
                              in_=grouped[:].rearrange("p o q j -> p (o q j)"))
        query_cols, gout_cols = slice(0, Q), slice(Q, 2 * Q)

        def product(dst, row_cols, slot_words, slot_scales, bank_tag):
            acc = ps.tile(dst.shape, F32, name=bank_tag)
            nc.tensor.matmul_mx(out=acc[:], lhsT=row_words[:, row_cols].bitcast(FP8X4),
                                lhsT_scale=row_scales[:, row_cols], rhs=slot_words.bitcast(FP8X4),
                                rhs_scale=slot_scales, start=True, stop=True)
            nc.scalar.copy(dst, acc[:])

        for h in range(R // BANK):
            cols = slice(h * BANK, (h + 1) * BANK)
            product(a_sb[:, cols], query_cols, key_words[:, cols], key_scales[:, cols], "a%d" % h)

        exp_bias = sb.tile([P, 1], F32)
        nc.scalar.activation(exp_bias[:], lse_t[:], ACT.Copy, scale=-1.0, bias=math.log(512.0))

        fade_turned = ps.tile([P, P], F32)
        nc.tensor.transpose(fade_turned[:], fade_rows[:], ident[:])
        fade_cols = sb.tile([P, BLOCKS], F32)
        nc.scalar.copy(fade_cols[:], fade_turned[:, :BLOCKS])

        for c0, c1 in VALUE_PIECES:
            val_words = sb.tile([P, c1 - c0], U32, align_bytes=64, name="val_words%d" % c0)
            nc.vector.tensor_copy(val_words[:],
                                  val_word_pool[:].indirect(offs_t[:, c0 // LIST_ROWS : c1 // LIST_ROWS]))
            product(dp_sb[:, c0:c1], gout_cols, val_words[:], val_scales[:, c0:c1], "dp%d" % c0)

        a_picked = sb.tile([P, I], F32, align_bytes=64, name="val_words%d" % VALUE_PIECES[0][0])
        weights = sb.tile([P, I], F32)
        nc.vector.tensor_copy(a_picked[:], a_sb[:].indirect(offs2_t[:]))
        nc.scalar.activation(weights[:], a_picked[:], ACT.Exp, bias=exp_bias[:])
        centred = sb.tile([P, I], F32)
        nc.vector.tensor_tensor(centred[:], dp_sb[:].indirect(offs2_t[:]), delta_wide[:], ALU.subtract)
        nc.vector.tensor_tensor(df[:].indirect(offs2_t[:]), centred[:], weights[:], ALU.mult)

        old_turned = []
        for h in range(R // BANK):
            turned_bank = ps.tile([P, BLOCKS_A_BANK, Q], F32, name="dp%d" % VALUE_PIECES[h + 1][0])
            for c in range(BLOCKS_A_BANK):
                b = h * BLOCKS_A_BANK + c
                nc.tensor.transpose(turned_bank[:, c, :], old_t[:, b * P : (b + 1) * P], ident[:])
            old_turned.append(turned_bank)
        faded_turned = sb.tile([P, BLOCKS, Q], F32, tag="a_then_faded")
        faded = []
        for h in range(R // BANK):
            faded_bank = ps.tile([P, BANK], F32, name="a%d" % h)
            for c in range(BLOCKS_A_BANK):
                b = h * BLOCKS_A_BANK + c
                nc.scalar.activation(faded_turned[:, b, :], old_turned[h][:, c, :], ACT.Copy,
                                     scale=fade_cols[:, b : b + 1])
                nc.tensor.transpose(faded_bank[:, c * P : (c + 1) * P], faded_turned[:, b, :], ident[:])
            faded.append(faded_bank)

        for piece in range(R // STORE_COLUMNS):
            c0 = piece * STORE_COLUMNS
            in_bank = c0 % BANK
            result = sb.tile([P, STORE_COLUMNS], F32, name="result%d" % piece)
            nc.vector.tensor_tensor(result[:], df[:, c0 : c0 + STORE_COLUMNS],
                                    faded[c0 // BANK][:, in_bank : in_bank + STORE_COLUMNS], ALU.add)
            queue = (nc.sync, nc.scalar)[piece % 2]
            queue.dma_start(out[:, c0 : c0 + STORE_COLUMNS], result[:])
